import numpy as np
import ml_dtypes


def mxq(x, axis, fmt="e4m3"):
    dtype, down = {"e4m3": (ml_dtypes.float8_e4m3fn, 7), "e5m2": (ml_dtypes.float8_e5m2, 14)}[fmt]
    v = np.moveaxis(np.asarray(x, np.float32).astype(ml_dtypes.bfloat16).astype(np.float64), axis, -1)
    blocks = v.reshape(v.shape[:-1] + (-1, 32))
    amax = np.abs(blocks).max(-1, keepdims=True)
    byte = np.maximum(np.where(amax > 0, np.frexp(amax)[1] - 1 + 127, 0) - down, 1)
    scale = np.exp2(byte - 127.0)
    codes = (blocks / scale).astype(np.float32).astype(dtype).astype(np.float64)
    return np.moveaxis((codes * scale).reshape(v.shape), -1, axis)


WIDE = False


def mx_kscale(k):
    if not WIDE:
        return np.ones(k)
    levels = np.array([10, -10, 5, -5, 0])
    if k % 512:
        return np.exp2(np.random.permutation(np.resize(levels, k // 32))).repeat(32)
    a = np.empty((k // 512, 16))
    for p in range(k // 512):
        a[p, :8] = np.random.permutation(np.resize(levels, 8))
        for g in range(8):
            far = levels[np.abs(levels - a[p, g]) >= 10]
            a[p, g + 8] = far[np.random.randint(len(far))]
    return np.exp2(a.ravel()).repeat(32)


def f64(x):
    return np.asarray(x).astype(np.float64)


def striped8(idx):
    return np.asarray(idx).reshape(8, -1, 16).transpose(0, 2, 1).reshape(128, -1).astype(np.uint16)


def unstriped8(offs):
    return offs.reshape(8, 16, -1).transpose(0, 2, 1).reshape(8, -1).astype(np.int64)


def pick8(x, idx, run):
    r = np.arange(len(x))
    return x[r[:, None], idx[r % (8 * run) // run]]


E2M1 = np.array([0.0, 0.5, 1.0, 1.5, 2.0, 3.0, 4.0, 6.0, -0.0, -0.5, -1.0, -1.5, -2.0, -3.0, -4.0, -6.0])


def pack_weight(w, fmt):
    k, n = w.shape
    w = f64(np.asarray(w, np.float32).astype(ml_dtypes.bfloat16)).reshape(k // 32, 32, n)
    amax = np.abs(w).max(1)
    if fmt == "e4m3":
        byte = np.frexp(amax)[1] - 1 + 127 - 7
    else:
        mant, ex = np.frexp(amax / 6.0)
        byte = np.where(mant > 0.5, ex, ex - 1) + 127
    byte = np.clip(np.where(amax > 0, byte, 1), 1, 254)
    scaled = (w * np.exp2(127.0 - byte)[:, None, :]).reshape(k, n).astype(np.float32)
    by_word = np.ascontiguousarray(scaled.reshape(k // 512, 128, 4, n).transpose(0, 1, 3, 2))
    if fmt == "e4m3":
        words = by_word.astype(ml_dtypes.float8_e4m3fn).view(np.uint8)
    else:
        c = by_word.astype(ml_dtypes.float4_e2m1fn).view(np.uint8) & 0xF
        words = (c[..., 0::2] | (c[..., 1::2] << 4)).reshape(k // 512, 128, 2 * n)
    return np.ascontiguousarray(words), np.ascontiguousarray(byte.astype(np.uint8).reshape(k // 512, 16, n))


def unpack_weight(words, scales, fmt):
    g, _, n = scales.shape
    words = np.ascontiguousarray(words).reshape(g, 128, n, -1)
    if fmt == "e4m3":
        vals = words.view(ml_dtypes.float8_e4m3fn).astype(np.float64)
    else:
        nib = np.empty((g, 128, n, 4), np.uint8)
        nib[..., 0::2] = words & 0xF
        nib[..., 1::2] = words >> 4
        vals = E2M1[nib]
    vals = vals * np.repeat(np.exp2(scales.astype(np.float64) - 127.0), 8, axis=1)[..., None]
    return vals.transpose(0, 1, 3, 2).reshape(g * 512, n)


D, T, U, X, S, I, Q = 512, 1024, 1024, 1024, 1024, 512, 128


def setup_inputs():
    n = np.random.standard_normal
    idx = np.stack([np.random.permutation(T)[:I] for _ in range(8)])
    idx2 = np.stack([np.random.permutation(U)[:I] for _ in range(8)])
    idx3 = np.stack([np.random.permutation(X)[:I] for _ in range(8)])
    idx4 = np.stack([np.random.permutation(S)[:I] for _ in range(8)])
    idx5 = np.stack([np.random.permutation(S)[:I] for _ in range(8)])
    idx6 = np.stack([np.random.permutation(S)[:I] for _ in range(8)])
    fd = mx_kscale(D)
    keysp = pack_weight(n((D, T)) / fd[:, None], "e4m3")
    notesp = pack_weight(n((D, U)) / fd[:, None], "e2m1")
    usersp = pack_weight(n((D, X)) / fd[:, None], "e4m3")
    shelvesp = pack_weight(n((D, S)) / fd[:, None], "e2m1")
    return {
        "query": (n((D, Q)) * 1.0 / np.sqrt(D) * fd[:, None]).astype(np.float32),
        "keys_words": keysp[0],
        "keys_scales": keysp[1],
        "notes_words": notesp[0],
        "notes_scales": notesp[1],
        "users_words": usersp[0],
        "users_scales": usersp[1],
        "shelves_words": shelvesp[0],
        "shelves_scales": shelvesp[1],
        "offs": striped8(idx),
        "offs2": striped8(idx2),
        "offs3": striped8(idx3),
        "offs4": striped8(idx4),
        "offs5": striped8(idx5),
        "offs6": striped8(idx6),
    }


def reference(query, keys_words, keys_scales, notes_words, notes_scales, users_words, users_scales, shelves_words, shelves_scales, offs, offs2, offs3, offs4, offs5, offs6):
    idx = unstriped8(offs)
    idx2 = unstriped8(offs2)
    idx3 = unstriped8(offs3)
    idx4 = unstriped8(offs4)
    idx5 = unstriped8(offs5)
    idx6 = unstriped8(offs6)
    keysu = unpack_weight(keys_words, keys_scales, "e4m3")
    notesu = unpack_weight(notes_words, notes_scales, "e2m1")
    usersu = unpack_weight(users_words, users_scales, "e4m3")
    shelvesu = unpack_weight(shelves_words, shelves_scales, "e2m1")
    queryq = mxq(f64(query), 0, "e4m3")
    a = queryq.T @ keysu
    b = queryq.T @ notesu
    c0 = queryq.T @ usersu
    d0 = queryq.T @ shelvesu
    w = pick8(a, idx, 16) - pick8(b, idx2, 16)
    v = pick8(c0, idx3, 16) - pick8(d0, idx4, 16)
    r = np.maximum(w, v)
    f1 = np.zeros((Q, S))
    f1[np.arange(Q)[:, None], idx5[np.arange(Q) % 128 // 16]] = r
    dd = d0 + f1
    y = pick8(dd, idx6, 16) - w
    return y

@@ -1,0 +1,134 @@
+from contextlib import ExitStack
+
+import concourse.mybir as mybir
+
+D, T, I, Q = 512, 1024, 512, 128
+FLOPS = 4 * 2 * D * T * Q
+
+F32 = mybir.dt.float32
+BF16 = mybir.dt.bfloat16
+I32 = mybir.dt.int32
+U32 = mybir.dt.uint32
+U16 = mybir.dt.uint16
+U8 = mybir.dt.uint8
+FP8X4 = mybir.dt.float8_e4m3fn_x4
+FP4X4 = mybir.dt.float4_e2m1fn_x4
+ALU = mybir.AluOpType
+COPY = mybir.ActivationFunctionType.Copy
+
+P = 128
+PACK = 4
+BANK = 512
+HALF = I // 2
+LIST_COLS = I // 16
+
+
+def tile_attend_fourway_four_kernel(tc, query, keys_words, keys_scales, notes_words, notes_scales,
+                                     users_words, users_scales, shelves_words, shelves_scales,
+                                     offs, offs2, offs3, offs4, offs5, offs6, out):
+    nc = tc.nc
+    with ExitStack() as ctx:
+        sb = ctx.enter_context(tc.tile_pool(name="sb", bufs=1))
+        ps = ctx.enter_context(tc.psum_pool(name="ps", bufs=1))
+
+        def load_list(name, src):
+            lst = sb.tile([P, LIST_COLS], U16, name=name)
+            nc.sync.dma_start(lst[:], src)
+            return lst
+
+        def load_words(name, src, row_bytes):
+            words = sb.tile([P, row_bytes], U8, name=name, align_bytes=64)
+            nc.sync.dma_start(out=words[:].bitcast(I32), in_=src.bitcast(I32))
+            return words
+
+        def load_scales(name, src, queue):
+            plane = sb.tile([P, T], U8, name=name, align_bytes=64)
+            for quad in range(4):
+                queue.dma_start(out=plane[32 * quad:32 * quad + 4, :].bitcast(I32),
+                                in_=src[0, 4 * quad:4 * quad + 4, :].bitcast(I32))
+            return plane
+
+        q_raw = sb.tile([P, PACK, Q], F32, name="q_raw")
+        nc.sync.dma_start(out=q_raw[:], in_=query.rearrange("(p j) q -> p j q", j=PACK))
+        notes_s = load_scales("notes_s", notes_scales, nc.sync)
+        notes_w = load_words("notes_w", notes_words[0], 2 * T)
+        keys_w = load_words("keys_w", keys_words[0].rearrange("p n t -> p (n t)"), 4 * T)
+        keys_s = load_scales("keys_s", keys_scales, nc.sync)
+        shelves_s = load_scales("shelves_s", shelves_scales, nc.gpsimd)
+        by_note = load_list("by_note", offs2)
+        shelves_w = load_words("shelves_w", shelves_words[0], 2 * T)
+        users_w = load_words("users_w", users_words[0].rearrange("p n t -> p (n t)"), 4 * T)
+        by_token = load_list("by_token", offs)
+        users_s = load_scales("users_s", users_scales, nc.sync)
+        by_shelf = load_list("by_shelf", offs4)
+        by_user = load_list("by_user", offs3)
+        put_at = load_list("put_at", offs5)
+        read_at = load_list("read_at", offs6)
+
+        f1 = sb.tile([P, T], F32, name="f1")
+        nc.vector.memset(f1[:], 0.0)
+
+        q_bf = sb.tile([P, Q, PACK], BF16, name="q_bf", align_bytes=64)
+        nc.vector.tensor_copy(
+            out=q_bf[:].rearrange("p (c i) t -> p c t i", i=4),
+            in_=q_raw[:].rearrange("p t (c i) -> p c t i", i=4))
+        q_codes = sb.tile([P, Q], U32, name="q_codes", align_bytes=64)
+        q_scales = sb.tile([P, Q], U8, name="q_scales", align_bytes=64)
+        nc.vector.quantize_mx(out=q_codes[:].bitcast(FP8X4), scales=q_scales[:],
+                              in_=q_bf[:].rearrange("p q t -> p (q t)"))
+
+        def scores(name, words, plane, x4, word_bytes):
+            table = sb.tile([P, T], F32, name=name)
+            for h in range(T // BANK):
+                bank = ps.tile([P, BANK], F32, name=name + "_bank%d" % h)
+                nc.tensor.matmul_mx(
+                    out=bank[:], lhsT=q_codes[:].bitcast(FP8X4), lhsT_scale=q_scales[:],
+                    rhs=words[:, word_bytes * BANK * h:word_bytes * BANK * (h + 1)].bitcast(x4),
+                    rhs_scale=plane[:, BANK * h:BANK * (h + 1)], start=True, stop=True)
+                nc.scalar.copy(out=table[:, BANK * h:BANK * (h + 1)], in_=bank[:])
+            return table
+
+        def slots(h):
+            return slice(HALF * h, HALF * (h + 1))
+
+        def part(lst, h):
+            return lst[:, LIST_COLS // 2 * h:LIST_COLS // 2 * (h + 1)]
+
+        b = scores("b", notes_w, notes_s, FP4X4, 2)
+        a = scores("a", keys_w, keys_s, FP8X4, 4)
+        d0 = scores("d0", shelves_w, shelves_s, FP4X4, 2)
+        c0 = scores("c0", users_w, users_s, FP8X4, 4)
+
+        b_g = sb.tile([P, I], F32, name="b_g")
+        nc.vector.tensor_copy(b_g[:], b[:].indirect(by_note[:]))
+        w = sb.tile([P, I], F32, name="w")
+        nc.vector.tensor_tensor(w[:], a[:].indirect(by_token[:]), b_g[:], ALU.subtract)
+
+        d_g0 = sb.tile([P, HALF], F32, name="d_g0")
+        d_g1 = sb.tile([P, HALF], F32, name="d_g1")
+        c_g1 = sb.tile([P, HALF], F32, name="c_g1")
+        v0 = sb.tile([P, HALF], F32, name="v0")
+        v1 = sb.tile([P, HALF], F32, name="v1")
+        r0 = sb.tile([P, HALF], F32, name="r0")
+        r1 = sb.tile([P, HALF], F32, name="r1")
+        nc.vector.tensor_copy(d_g0[:], d0[:].indirect(part(by_shelf, 0)))
+        nc.vector.tensor_tensor(v0[:], c0[:].indirect(part(by_user, 0)), d_g0[:], ALU.subtract)
+        nc.scalar.activation(d_g1[:], d0[:].indirect(part(by_shelf, 1)), COPY)
+        nc.scalar.activation(c_g1[:], c0[:].indirect(part(by_user, 1)), COPY)
+        nc.vector.tensor_tensor(r0[:], w[:, slots(0)], v0[:], ALU.max)
+        nc.vector.tensor_copy(f1[:].indirect(part(put_at, 0)), r0[:])
+        nc.vector.tensor_tensor(v1[:], c_g1[:], d_g1[:], ALU.subtract)
+        nc.vector.tensor_tensor(r1[:], w[:, slots(1)], v1[:], ALU.max)
+        nc.vector.tensor_copy(f1[:].indirect(part(put_at, 1)), r1[:])
+
+        dd = sb.tile([P, T], F32, name="dd")
+        nc.vector.tensor_tensor(dd[:], d0[:], f1[:], ALU.add)
+
+        y0 = sb.tile([P, HALF], F32, name="y0")
+        y1 = sb.tile([P, HALF], F32, name="y1")
+        dd_g1 = sb.tile([P, HALF], F32, name="dd_g1")
+        nc.vector.tensor_tensor(y0[:], dd[:].indirect(part(read_at, 0)), w[:, slots(0)], ALU.subtract)
+        nc.scalar.activation(dd_g1[:], dd[:].indirect(part(read_at, 1)), COPY)
+        nc.sync.dma_start(out=out[:, slots(0)], in_=y0[:])
+        nc.vector.tensor_tensor(y1[:], dd_g1[:], w[:, slots(1)], ALU.subtract)
+        nc.scalar.dma_start(out=out[:, slots(1)], in_=y1[:])

@@ -36,46 +36,52 @@ def tile_attend_fourway_four_kernel(tc, query, keys_words, keys_scales, notes_wo
             nc.sync.dma_start(lst[:], src)
             return lst
 
-        def load_words(name, src, row_bytes):
+        def load_words(name, src, row_bytes, queue):
             words = sb.tile([P, row_bytes], U8, name=name, align_bytes=64)
-            nc.sync.dma_start(out=words[:].bitcast(I32), in_=src.bitcast(I32))
+            queue.dma_start(out=words[:].bitcast(I32), in_=src.bitcast(I32))
             return words
 
-        def load_scales(name, src, queue):
-            plane = sb.tile([P, T], U8, name=name, align_bytes=64)
-            for quad in range(4):
+        def scale_plane(name):
+            return sb.tile([P, T], U8, name=name, align_bytes=64)
+
+        def load_scale_rows(plane, src, quads, queue):
+            for quad in quads:
                 queue.dma_start(out=plane[32 * quad:32 * quad + 4, :].bitcast(I32),
                                 in_=src[0, 4 * quad:4 * quad + 4, :].bitcast(I32))
-            return plane
 
         q_raw = sb.tile([P, PACK, Q], F32, name="q_raw")
         nc.sync.dma_start(out=q_raw[:], in_=query.rearrange("(p j) q -> p j q", j=PACK))
-        notes_s = load_scales("notes_s", notes_scales, nc.sync)
-        notes_w = load_words("notes_w", notes_words[0], 2 * T)
-        keys_w = load_words("keys_w", keys_words[0].rearrange("p n t -> p (n t)"), 4 * T)
-        keys_s = load_scales("keys_s", keys_scales, nc.sync)
-        shelves_s = load_scales("shelves_s", shelves_scales, nc.gpsimd)
+        notes_s, keys_s = scale_plane("notes_s"), scale_plane("keys_s")
+        shelves_s, users_s = scale_plane("shelves_s"), scale_plane("users_s")
+        keys_w = load_words("keys_w", keys_words[0].rearrange("p n t -> p (n t)"), 4 * T, nc.gpsimd)
+        shelves_w = load_words("shelves_w", shelves_words[0], 2 * T, nc.gpsimd)
+        users_w = load_words("users_w", users_words[0].rearrange("p n t -> p (n t)"), 4 * T, nc.gpsimd)
+        load_scale_rows(notes_s, notes_scales, range(4), nc.sync)
+        notes_w = load_words("notes_w", notes_words[0], 2 * T, nc.sync)
+        load_scale_rows(keys_s, keys_scales, range(4), nc.sync)
         by_note = load_list("by_note", offs2)
-        shelves_w = load_words("shelves_w", shelves_words[0], 2 * T)
-        users_w = load_words("users_w", users_words[0].rearrange("p n t -> p (n t)"), 4 * T)
+        load_scale_rows(shelves_s, shelves_scales, range(4), nc.sync)
         by_token = load_list("by_token", offs)
-        users_s = load_scales("users_s", users_scales, nc.sync)
+        load_scale_rows(users_s, users_scales, range(4), nc.sync)
         by_shelf = load_list("by_shelf", offs4)
         by_user = load_list("by_user", offs3)
         put_at = load_list("put_at", offs5)
         read_at = load_list("read_at", offs6)
 
-        f1 = sb.tile([P, T], F32, name="f1")
-        nc.vector.memset(f1[:], 0.0)
-
-        q_bf = sb.tile([P, Q, PACK], BF16, name="q_bf", align_bytes=64)
-        nc.vector.tensor_copy(
-            out=q_bf[:].rearrange("p (c i) t -> p c t i", i=4),
-            in_=q_raw[:].rearrange("p t (c i) -> p c t i", i=4))
+        q_bf = sb.tile([P, Q, PACK], BF16, name="q_bf", tag="q_bf_then_f1", align_bytes=64)
         q_codes = sb.tile([P, Q], U32, name="q_codes", align_bytes=64)
         q_scales = sb.tile([P, Q], U8, name="q_scales", align_bytes=64)
-        nc.vector.quantize_mx(out=q_codes[:].bitcast(FP8X4), scales=q_scales[:],
-                              in_=q_bf[:].rearrange("p q t -> p (q t)"))
+        q_halves = [slice(0, Q // 2), slice(Q // 2, Q)]
+        for cols in q_halves:
+            nc.vector.tensor_copy(
+                out=q_bf[:, cols, :].rearrange("p (c i) t -> p c t i", i=4),
+                in_=q_raw[:, :, cols].rearrange("p t (c i) -> p c t i", i=4))
+        for cols in q_halves:
+            nc.vector.quantize_mx(out=q_codes[:, cols].bitcast(FP8X4), scales=q_scales[:, cols],
+                                  in_=q_bf[:, cols, :].rearrange("p q t -> p (q t)"))
+
+        f1 = sb.tile([P, T], F32, name="f1", tag="q_bf_then_f1", align_bytes=64)
+        nc.vector.memset(f1[:], 0.0)
 
         def scores(name, words, plane, x4, word_bytes):
             table = sb.tile([P, T], F32, name=name)
@@ -116,8 +122,8 @@ def tile_attend_fourway_four_kernel(tc, query, keys_words, keys_scales, notes_wo
         nc.scalar.activation(d_g1[:], d0[:].indirect(part(by_shelf, 1)), COPY)
         nc.scalar.activation(c_g1[:], c0[:].indirect(part(by_user, 1)), COPY)
         nc.vector.tensor_tensor(r0[:], w[:, slots(0)], v0[:], ALU.max)
-        nc.vector.tensor_copy(f1[:].indirect(part(put_at, 0)), r0[:])
         nc.vector.tensor_tensor(v1[:], c_g1[:], d_g1[:], ALU.subtract)
+        nc.vector.tensor_copy(f1[:].indirect(part(put_at, 0)), r0[:])
         nc.vector.tensor_tensor(r1[:], w[:, slots(1)], v1[:], ALU.max)
         nc.vector.tensor_copy(f1[:].indirect(part(put_at, 1)), r1[:])
 

@@ -36,9 +36,12 @@ def tile_attend_fourway_four_kernel(tc, query, keys_words, keys_scales, notes_wo
             nc.sync.dma_start(lst[:], src)
             return lst
 
-        def load_words(name, src, row_bytes, queue):
+        def load_words(name, src, row_bytes, queue, pieces=1):
             words = sb.tile([P, row_bytes], U8, name=name, align_bytes=64)
-            queue.dma_start(out=words[:].bitcast(I32), in_=src.bitcast(I32))
+            step = row_bytes // pieces
+            for n in range(pieces):
+                queue.dma_start(out=words[:, step * n:step * (n + 1)].bitcast(I32),
+                                in_=src[:, step * n:step * (n + 1)].bitcast(I32))
             return words
 
         def scale_plane(name):
@@ -55,7 +58,7 @@ def tile_attend_fourway_four_kernel(tc, query, keys_words, keys_scales, notes_wo
         shelves_s, users_s = scale_plane("shelves_s"), scale_plane("users_s")
         keys_w = load_words("keys_w", keys_words[0].rearrange("p n t -> p (n t)"), 4 * T, nc.gpsimd)
         shelves_w = load_words("shelves_w", shelves_words[0], 2 * T, nc.gpsimd)
-        users_w = load_words("users_w", users_words[0].rearrange("p n t -> p (n t)"), 4 * T, nc.gpsimd)
+        users_w = load_words("users_w", users_words[0].rearrange("p n t -> p (n t)"), 4 * T, nc.gpsimd, 2)
         load_scale_rows(notes_s, notes_scales, range(4), nc.sync)
         notes_w = load_words("notes_w", notes_words[0], 2 * T, nc.sync)
         load_scale_rows(keys_s, keys_scales, range(4), nc.sync)
@@ -85,14 +88,16 @@ def tile_attend_fourway_four_kernel(tc, query, keys_words, keys_scales, notes_wo
 
         def scores(name, words, plane, x4, word_bytes):
             table = sb.tile([P, T], F32, name=name)
+            banks = []
             for h in range(T // BANK):
                 bank = ps.tile([P, BANK], F32, name=name + "_bank%d" % h)
                 nc.tensor.matmul_mx(
                     out=bank[:], lhsT=q_codes[:].bitcast(FP8X4), lhsT_scale=q_scales[:],
                     rhs=words[:, word_bytes * BANK * h:word_bytes * BANK * (h + 1)].bitcast(x4),
                     rhs_scale=plane[:, BANK * h:BANK * (h + 1)], start=True, stop=True)
+                banks.append(bank)
                 nc.scalar.copy(out=table[:, BANK * h:BANK * (h + 1)], in_=bank[:])
-            return table
+            return table, banks
 
         def slots(h):
             return slice(HALF * h, HALF * (h + 1))
@@ -100,10 +105,10 @@ def tile_attend_fourway_four_kernel(tc, query, keys_words, keys_scales, notes_wo
         def part(lst, h):
             return lst[:, LIST_COLS // 2 * h:LIST_COLS // 2 * (h + 1)]
 
-        b = scores("b", notes_w, notes_s, FP4X4, 2)
-        a = scores("a", keys_w, keys_s, FP8X4, 4)
-        d0 = scores("d0", shelves_w, shelves_s, FP4X4, 2)
-        c0 = scores("c0", users_w, users_s, FP8X4, 4)
+        b, b_banks = scores("b", notes_w, notes_s, FP4X4, 2)
+        a, a_banks = scores("a", keys_w, keys_s, FP8X4, 4)
+        d0, d_banks = scores("d0", shelves_w, shelves_s, FP4X4, 2)
+        c0, c_banks = scores("c0", users_w, users_s, FP8X4, 4)
 
         b_g = sb.tile([P, I], F32, name="b_g")
         nc.vector.tensor_copy(b_g[:], b[:].indirect(by_note[:]))
@@ -128,7 +133,10 @@ def tile_attend_fourway_four_kernel(tc, query, keys_words, keys_scales, notes_wo
         nc.vector.tensor_copy(f1[:].indirect(part(put_at, 1)), r1[:])
 
         dd = sb.tile([P, T], F32, name="dd")
-        nc.vector.tensor_tensor(dd[:], d0[:], f1[:], ALU.add)
+        cut = T - 256
+        nc.gpsimd.tensor_tensor(dd[:, cut:T], d0[:, cut:T], f1[:, cut:T], ALU.add)
+        nc.vector.tensor_tensor(dd[:, 0:BANK], d_banks[0][:], f1[:, 0:BANK], ALU.add)
+        nc.vector.tensor_tensor(dd[:, BANK:cut], d_banks[1][:, 0:cut - BANK], f1[:, BANK:cut], ALU.add)
 
         y0 = sb.tile([P, HALF], F32, name="y0")
         y1 = sb.tile([P, HALF], F32, name="y1")

from contextlib import ExitStack

import concourse.mybir as mybir

D, T, I, Q = 512, 1024, 512, 128
FLOPS = 4 * 2 * D * T * Q

F32 = mybir.dt.float32
BF16 = mybir.dt.bfloat16
I32 = mybir.dt.int32
U32 = mybir.dt.uint32
U16 = mybir.dt.uint16
U8 = mybir.dt.uint8
FP8X4 = mybir.dt.float8_e4m3fn_x4
FP4X4 = mybir.dt.float4_e2m1fn_x4
ALU = mybir.AluOpType
COPY = mybir.ActivationFunctionType.Copy

P = 128
PACK = 4
BANK = 512
HALF = I // 2
LIST_COLS = I // 16


def tile_attend_fourway_four_kernel(tc, query, keys_words, keys_scales, notes_words, notes_scales,
                                     users_words, users_scales, shelves_words, shelves_scales,
                                     offs, offs2, offs3, offs4, offs5, offs6, out):
    nc = tc.nc
    with ExitStack() as ctx:
        sb = ctx.enter_context(tc.tile_pool(name="sb", bufs=1))
        ps = ctx.enter_context(tc.psum_pool(name="ps", bufs=1))

        def load_list(name, src):
            lst = sb.tile([P, LIST_COLS], U16, name=name)
            nc.sync.dma_start(lst[:], src)
            return lst

        def load_words(name, src, row_bytes, queue, pieces=1):
            words = sb.tile([P, row_bytes], U8, name=name, align_bytes=64)
            step = row_bytes // pieces
            for n in range(pieces):
                queue.dma_start(out=words[:, step * n:step * (n + 1)].bitcast(I32),
                                in_=src[:, step * n:step * (n + 1)].bitcast(I32))
            return words

        def scale_plane(name):
            return sb.tile([P, T], U8, name=name, align_bytes=64)

        def load_scale_rows(plane, src, quads, queue):
            for quad in quads:
                queue.dma_start(out=plane[32 * quad:32 * quad + 4, :].bitcast(I32),
                                in_=src[0, 4 * quad:4 * quad + 4, :].bitcast(I32))

        q_raw = sb.tile([P, PACK, Q], F32, name="q_raw")
        nc.sync.dma_start(out=q_raw[:], in_=query.rearrange("(p j) q -> p j q", j=PACK))
        notes_s, keys_s = scale_plane("notes_s"), scale_plane("keys_s")
        shelves_s, users_s = scale_plane("shelves_s"), scale_plane("users_s")
        keys_w = load_words("keys_w", keys_words[0].rearrange("p n t -> p (n t)"), 4 * T, nc.gpsimd)
        shelves_w = load_words("shelves_w", shelves_words[0], 2 * T, nc.gpsimd)
        users_w = load_words("users_w", users_words[0].rearrange("p n t -> p (n t)"), 4 * T, nc.gpsimd, 2)
        load_scale_rows(notes_s, notes_scales, range(4), nc.sync)
        notes_w = load_words("notes_w", notes_words[0], 2 * T, nc.sync)
        load_scale_rows(keys_s, keys_scales, range(4), nc.sync)
        by_note = load_list("by_note", offs2)
        load_scale_rows(shelves_s, shelves_scales, range(4), nc.sync)
        by_token = load_list("by_token", offs)
        load_scale_rows(users_s, users_scales, range(4), nc.sync)
        by_shelf = load_list("by_shelf", offs4)
        by_user = load_list("by_user", offs3)
        put_at = load_list("put_at", offs5)
        read_at = load_list("read_at", offs6)

        q_bf = sb.tile([P, Q, PACK], BF16, name="q_bf", tag="q_bf_then_f1", align_bytes=64)
        q_codes = sb.tile([P, Q], U32, name="q_codes", align_bytes=64)
        q_scales = sb.tile([P, Q], U8, name="q_scales", align_bytes=64)
        q_halves = [slice(0, Q // 2), slice(Q // 2, Q)]
        for cols in q_halves:
            nc.vector.tensor_copy(
                out=q_bf[:, cols, :].rearrange("p (c i) t -> p c t i", i=4),
                in_=q_raw[:, :, cols].rearrange("p t (c i) -> p c t i", i=4))
        for cols in q_halves:
            nc.vector.quantize_mx(out=q_codes[:, cols].bitcast(FP8X4), scales=q_scales[:, cols],
                                  in_=q_bf[:, cols, :].rearrange("p q t -> p (q t)"))

        f1 = sb.tile([P, T], F32, name="f1", tag="q_bf_then_f1", align_bytes=64)
        nc.vector.memset(f1[:], 0.0)

        def scores(name, words, plane, x4, word_bytes):
            table = sb.tile([P, T], F32, name=name)
            banks = []
            for h in range(T // BANK):
                bank = ps.tile([P, BANK], F32, name=name + "_bank%d" % h)
                nc.tensor.matmul_mx(
                    out=bank[:], lhsT=q_codes[:].bitcast(FP8X4), lhsT_scale=q_scales[:],
                    rhs=words[:, word_bytes * BANK * h:word_bytes * BANK * (h + 1)].bitcast(x4),
                    rhs_scale=plane[:, BANK * h:BANK * (h + 1)], start=True, stop=True)
                banks.append(bank)
                nc.scalar.copy(out=table[:, BANK * h:BANK * (h + 1)], in_=bank[:])
            return table, banks

        def slots(h):
            return slice(HALF * h, HALF * (h + 1))

        def part(lst, h):
            return lst[:, LIST_COLS // 2 * h:LIST_COLS // 2 * (h + 1)]

        b, b_banks = scores("b", notes_w, notes_s, FP4X4, 2)
        a, a_banks = scores("a", keys_w, keys_s, FP8X4, 4)
        d0, d_banks = scores("d0", shelves_w, shelves_s, FP4X4, 2)
        c0, c_banks = scores("c0", users_w, users_s, FP8X4, 4)

        b_g = sb.tile([P, I], F32, name="b_g")
        nc.vector.tensor_copy(b_g[:], b[:].indirect(by_note[:]))
        w = sb.tile([P, I], F32, name="w")
        nc.vector.tensor_tensor(w[:], a[:].indirect(by_token[:]), b_g[:], ALU.subtract)

        d_g0 = sb.tile([P, HALF], F32, name="d_g0")
        d_g1 = sb.tile([P, HALF], F32, name="d_g1")
        c_g1 = sb.tile([P, HALF], F32, name="c_g1")
        v0 = sb.tile([P, HALF], F32, name="v0")
        v1 = sb.tile([P, HALF], F32, name="v1")
        r0 = sb.tile([P, HALF], F32, name="r0")
        r1 = sb.tile([P, HALF], F32, name="r1")
        nc.vector.tensor_copy(d_g0[:], d0[:].indirect(part(by_shelf, 0)))
        nc.vector.tensor_tensor(v0[:], c0[:].indirect(part(by_user, 0)), d_g0[:], ALU.subtract)
        nc.scalar.activation(d_g1[:], d0[:].indirect(part(by_shelf, 1)), COPY)
        nc.scalar.activation(c_g1[:], c0[:].indirect(part(by_user, 1)), COPY)
        nc.vector.tensor_tensor(r0[:], w[:, slots(0)], v0[:], ALU.max)
        nc.vector.tensor_tensor(v1[:], c_g1[:], d_g1[:], ALU.subtract)
        nc.vector.tensor_copy(f1[:].indirect(part(put_at, 0)), r0[:])
        nc.vector.tensor_tensor(r1[:], w[:, slots(1)], v1[:], ALU.max)
        nc.vector.tensor_copy(f1[:].indirect(part(put_at, 1)), r1[:])

        dd = sb.tile([P, T], F32, name="dd")
        cut = T - 256
        nc.gpsimd.tensor_tensor(dd[:, cut:T], d0[:, cut:T], f1[:, cut:T], ALU.add)
        nc.vector.tensor_tensor(dd[:, 0:BANK], d_banks[0][:], f1[:, 0:BANK], ALU.add)
        nc.vector.tensor_tensor(dd[:, BANK:cut], d_banks[1][:, 0:cut - BANK], f1[:, BANK:cut], ALU.add)

        y0 = sb.tile([P, HALF], F32, name="y0")
        y1 = sb.tile([P, HALF], F32, name="y1")
        dd_g1 = sb.tile([P, HALF], F32, name="dd_g1")
        nc.vector.tensor_tensor(y0[:], dd[:].indirect(part(read_at, 0)), w[:, slots(0)], ALU.subtract)
        nc.scalar.activation(dd_g1[:], dd[:].indirect(part(read_at, 1)), COPY)
        nc.sync.dma_start(out=out[:, slots(0)], in_=y0[:])
        nc.vector.tensor_tensor(y1[:], dd_g1[:], w[:, slots(1)], ALU.subtract)
        nc.scalar.dma_start(out=out[:, slots(1)], in_=y1[:])
